import numpy as np
CORES = [66,67,70,71,194,195,198,199]
N = 8
def setup_inputs(rng):
    return {"x": rng.standard_normal((N, 128, 2048), dtype=np.float32)}
def reference(x):
    b = 2048 // N
    blocks = x.reshape(N, 128, N, b)
    return {"y": np.ascontiguousarray(blocks.transpose(2, 1, 0, 3)).reshape(N, 128, 2048)}

@@ -1,0 +1,135 @@
+from concourse.bass import DstId, RemoteDMATransfer
+
+B = 256
+
+PIECES = [
+    ("R", 0, 0, 256),
+    ("D", 1, 0, 256),
+    ("D", 2, 0, 256),
+    ("D", 3, 0, 256),
+]
+CALLS = [
+    [(0, 0x0F), (1, 0xF0)],
+    [(2, 0x0F), (3, 0xF0)],
+]
+HELP_MASK = 0xFF
+LOADS = [("sync", 0), ("scalar", 1), ("sync", 2), ("scalar", 3)]
+OC_MASK = {1: 0x0F00, 2: 0x3000, 3: 0xC000}
+STORES = [
+    ("sync", 1, 0, 256, [1]),
+    ("scalar", 0, 0, 256, [0]),
+    ("sync", 2, 0, 256, [2]),
+    ("scalar", 3, 0, 256, [3]),
+]
+
+SCRATCH = {
+    "stage": ("sbuf", [128, 2048], "float32"),
+    "land": ("sbuf", [128, 2048], "float32"),
+}
+SEMAPHORES = (["l%d" % k for k in range(4)] + ["a%d" % p for p in range(len(PIECES))]
+              + ["lo", "oc", "sent", "st"])
+
+
+def popc(m):
+    return bin(m).count("1")
+
+
+def piece_mask():
+    d = {}
+    for call in CALLS:
+        for p, m in call:
+            d[p] = m
+    return d
+
+
+def helper_of(core):
+    return (1 - core // 128) * 128 + 72 + core % 8
+
+
+def helper_program(g, core, T, topo, s):
+    pm = piece_mask()
+    hs, i = s // 4, s % 4
+    total = 0
+    for call in CALLS:
+        for p, m in call:
+            way, k, c0, c1 = PIECES[p]
+            if way != "R":
+                continue
+            d = T.cores[4 * (1 - hs) + (i + k) % 4]
+            ap = T.land[:, s * B + c0:s * B + c1]
+            sem = T.sem["a%d" % p]
+            g.wait_ge(sem, popc(pm[p]))
+            rid, pnc = topo.addr(d, core)
+            g.remote_dma(out_ap=ap, in_ap=ap, remote_sem=sem, local_sem=T.sem.sent, pid=pnc, routing_id=rid,
+                         dma_engine_mask=HELP_MASK)
+            total += popc(HELP_MASK)
+    if total:
+        g.wait_ge(T.sem.sent, total)
+
+
+def rank_program(g, core, T, topo):
+    rank = T.rank_of(core)
+    if rank is None:
+        if topo.chip(core) == 9 and core % 8 in (2, 3, 6, 7):
+            helper_program(g, core, T, topo, T.rank_of((1 - core // 128) * 128 + 64 + core % 8))
+        return
+    h, i = rank // 4, rank % 4
+    far, near = 4 * (1 - h), 4 * h
+    q = {"sync": g.sync, "scalar": g.scalar}
+    pm = piece_mask()
+    nst = 0
+
+    for qn, k in LOADS:
+        d = far + (i + k) % 4
+        q[qn].dma_start(T.stage[:, d * B:(d + 1) * B], T.x[:, d * B:(d + 1) * B]).then_inc(T.sem["l%d" % k], 16)
+    near_ranges = [(a, e) for a, e in ((near, rank), (rank + 1, near + 4)) if e > a]
+    for n, (a, e) in enumerate(near_ranges):
+        q[("sync", "scalar")[n]].dma_start(T.stage[:, a * B:e * B], T.x[:, a * B:e * B]).then_inc(T.sem.lo, 16)
+    q["scalar" if len(near_ranges) == 1 else "sync"].dma_start(
+        T.y[:, rank * B:(rank + 1) * B], T.x[:, rank * B:(rank + 1) * B]).then_inc(T.sem.st, 16)
+    nst += 1
+
+    sent = 0
+    have = set()
+    mine = T.land[:, rank * B:(rank + 1) * B]
+    for call in CALLS:
+        trs = []
+        for p, m in call:
+            way, k, c0, c1 = PIECES[p]
+            if k not in have:
+                g.wait_ge(T.sem["l%d" % k], 16)
+                have.add(k)
+            d = far + (i + k) % 4
+            to = T.cores[d] if way == "D" else helper_of(core)
+            rid, pnc = topo.addr(to, core)
+            trs.append(RemoteDMATransfer(dst_ids=[DstId(rid=rid, pnc=pnc)], dma_engine_mask=m,
+                                         remote_sem=T.sem["a%d" % p],
+                                         src=T.stage[:, d * B + c0:d * B + c1],
+                                         dst=T.land[:, rank * B + c0:rank * B + c1]))
+            sent += popc(m)
+        g.remote_dma_fused(trs, local_sem=T.sem.sent)
+    g.wait_ge(T.sem.lo, 16 * len(near_ranges))
+    trs = []
+    for k in (1, 2, 3):
+        d = near + (i + k) % 4
+        rid, pnc = topo.addr(T.cores[d], core)
+        trs.append(RemoteDMATransfer(dst_ids=[DstId(rid=rid, pnc=pnc)], dma_engine_mask=OC_MASK[k], remote_sem=T.sem.oc,
+                                     src=T.stage[:, d * B:(d + 1) * B], dst=mine))
+        sent += popc(OC_MASK[k])
+    g.remote_dma_fused(trs, local_sem=T.sem.sent)
+
+    oc_total = sum(popc(m) for m in OC_MASK.values())
+    for n, (a, e) in enumerate(near_ranges):
+        qq = q[("sync", "scalar")[n]]
+        qq.wait_ge(T.sem.oc, oc_total)
+        qq.dma_start(T.y[:, a * B:e * B], T.land[:, a * B:e * B]).then_inc(T.sem.st, 16)
+        nst += 1
+    for qn, k, c0, c1, ps in STORES:
+        s = far + (i - k) % 4
+        for p in ps:
+            q[qn].wait_ge(T.sem["a%d" % p], popc(pm[p]) if PIECES[p][0] == "D" else popc(HELP_MASK))
+        q[qn].dma_start(T.y[:, s * B + c0:s * B + c1], T.land[:, s * B + c0:s * B + c1]).then_inc(T.sem.st, 16)
+        nst += 1
+
+    g.wait_ge(T.sem.sent, sent)
+    g.wait_ge(T.sem.st, 16 * nst)

@@ -3,23 +3,29 @@ from concourse.bass import DstId, RemoteDMATransfer
 B = 256
 
 PIECES = [
-    ("R", 0, 0, 256),
-    ("D", 1, 0, 256),
-    ("D", 2, 0, 256),
-    ("D", 3, 0, 256),
+    ("R", 0, 0, 128),
+    ("R", 0, 128, 256),
+    ("R", 1, 0, 128),
+    ("D", 1, 128, 256),
+    ("D", 2, 0, 128),
+    ("D", 2, 128, 256),
+    ("D", 3, 0, 128),
+    ("D", 3, 128, 256),
 ]
 CALLS = [
-    [(0, 0x0F), (1, 0xF0)],
-    [(2, 0x0F), (3, 0xF0)],
+    [(0, 0x0F), (3, 0x30), (4, 0xC0)],
+    [(1, 0x0F), (5, 0x30), (6, 0xC0)],
+    [(2, 0x0F), (7, 0xF0)],
+    {1: 0x0F00, 2: 0x3000, 3: 0xC000},
 ]
 HELP_MASK = 0xFF
-LOADS = [("sync", 0), ("scalar", 1), ("sync", 2), ("scalar", 3)]
-OC_MASK = {1: 0x0F00, 2: 0x3000, 3: 0xC000}
+LOADS = [("sync", "far")]
+NEAR_Q = ("scalar", "sync")
 STORES = [
-    ("sync", 1, 0, 256, [1]),
-    ("scalar", 0, 0, 256, [0]),
-    ("sync", 2, 0, 256, [2]),
-    ("scalar", 3, 0, 256, [3]),
+    ("sync", 2, 0, 256, [4, 5]),
+    ("scalar", 0, 0, 256, [0, 1]),
+    ("sync", 3, 0, 256, [6, 7]),
+    ("scalar", 1, 0, 256, [3, 2]),
 ]
 
 SCRATCH = {
@@ -27,16 +33,20 @@ SCRATCH = {
     "land": ("sbuf", [128, 2048], "float32"),
 }
 SEMAPHORES = (["l%d" % k for k in range(4)] + ["a%d" % p for p in range(len(PIECES))]
-              + ["lo", "oc", "sent", "st"])
+              + ["lo", "oc", "sent", "st", "gst"])
 
 
 def popc(m):
     return bin(m).count("1")
 
 
+def far_calls():
+    return [c for c in CALLS if not isinstance(c, dict)]
+
+
 def piece_mask():
     d = {}
-    for call in CALLS:
+    for call in far_calls():
         for p, m in call:
             d[p] = m
     return d
@@ -50,18 +60,17 @@ def helper_program(g, core, T, topo, s):
     pm = piece_mask()
     hs, i = s // 4, s % 4
     total = 0
-    for call in CALLS:
+    for call in far_calls():
         for p, m in call:
             way, k, c0, c1 = PIECES[p]
             if way != "R":
                 continue
-            d = T.cores[4 * (1 - hs) + (i + k) % 4]
-            ap = T.land[:, s * B + c0:s * B + c1]
+            d = 4 * (1 - hs) + (i + k) % 4
             sem = T.sem["a%d" % p]
             g.wait_ge(sem, popc(pm[p]))
-            rid, pnc = topo.addr(d, core)
-            g.remote_dma(out_ap=ap, in_ap=ap, remote_sem=sem, local_sem=T.sem.sent, pid=pnc, routing_id=rid,
-                         dma_engine_mask=HELP_MASK)
+            rid, pnc = topo.addr(T.cores[d], core)
+            g.remote_dma(out_ap=T.land[:, s * B + c0:s * B + c1], in_ap=T.land[:, d * B + c0:d * B + c1], remote_sem=sem,
+                         local_sem=T.sem.sent, pid=pnc, routing_id=rid, dma_engine_mask=HELP_MASK)
             total += popc(HELP_MASK)
     if total:
         g.wait_ge(T.sem.sent, total)
@@ -79,57 +88,72 @@ def rank_program(g, core, T, topo):
     pm = piece_mask()
     nst = 0
 
+    lsem = {}
     for qn, k in LOADS:
-        d = far + (i + k) % 4
-        q[qn].dma_start(T.stage[:, d * B:(d + 1) * B], T.x[:, d * B:(d + 1) * B]).then_inc(T.sem["l%d" % k], 16)
+        if k == "far":
+            a, e = far * B, (far + 4) * B
+            for kk in range(4):
+                lsem[kk] = "l0"
+        else:
+            a = (far + (i + k) % 4) * B
+            e = a + B
+            lsem[k] = "l%d" % k
+        q[qn].dma_start(T.stage[:, a:e], T.x[:, a:e]).then_inc(T.sem[lsem[0 if k == "far" else k]], 16)
     near_ranges = [(a, e) for a, e in ((near, rank), (rank + 1, near + 4)) if e > a]
     for n, (a, e) in enumerate(near_ranges):
-        q[("sync", "scalar")[n]].dma_start(T.stage[:, a * B:e * B], T.x[:, a * B:e * B]).then_inc(T.sem.lo, 16)
-    q["scalar" if len(near_ranges) == 1 else "sync"].dma_start(
+        q[NEAR_Q[n]].dma_start(T.stage[:, a * B:e * B], T.x[:, a * B:e * B]).then_inc(T.sem.lo, 16)
+    q[NEAR_Q[len(near_ranges) % 2]].dma_start(
         T.y[:, rank * B:(rank + 1) * B], T.x[:, rank * B:(rank + 1) * B]).then_inc(T.sem.st, 16)
     nst += 1
 
     sent = 0
+    oc_total = 0
     have = set()
     mine = T.land[:, rank * B:(rank + 1) * B]
     for call in CALLS:
         trs = []
+        if isinstance(call, dict):
+            if "lo" not in have:
+                g.wait_ge(T.sem.lo, 16 * len(near_ranges))
+                have.add("lo")
+            for k, m in call.items():
+                d = near + (i + k) % 4
+                rid, pnc = topo.addr(T.cores[d], core)
+                trs.append(RemoteDMATransfer(dst_ids=[DstId(rid=rid, pnc=pnc)], dma_engine_mask=m,
+                                             remote_sem=T.sem.oc, src=T.stage[:, d * B:(d + 1) * B], dst=mine))
+                sent += popc(m)
+                oc_total += popc(m)
+            g.remote_dma_fused(trs, local_sem=T.sem.sent)
+            continue
         for p, m in call:
             way, k, c0, c1 = PIECES[p]
-            if k not in have:
-                g.wait_ge(T.sem["l%d" % k], 16)
-                have.add(k)
+            if lsem[k] not in have:
+                g.wait_ge(T.sem[lsem[k]], 16)
+                have.add(lsem[k])
             d = far + (i + k) % 4
             to = T.cores[d] if way == "D" else helper_of(core)
+            at = rank if way == "D" else d
             rid, pnc = topo.addr(to, core)
             trs.append(RemoteDMATransfer(dst_ids=[DstId(rid=rid, pnc=pnc)], dma_engine_mask=m,
                                          remote_sem=T.sem["a%d" % p],
                                          src=T.stage[:, d * B + c0:d * B + c1],
-                                         dst=T.land[:, rank * B + c0:rank * B + c1]))
+                                         dst=T.land[:, at * B + c0:at * B + c1]))
             sent += popc(m)
         g.remote_dma_fused(trs, local_sem=T.sem.sent)
-    g.wait_ge(T.sem.lo, 16 * len(near_ranges))
-    trs = []
-    for k in (1, 2, 3):
-        d = near + (i + k) % 4
-        rid, pnc = topo.addr(T.cores[d], core)
-        trs.append(RemoteDMATransfer(dst_ids=[DstId(rid=rid, pnc=pnc)], dma_engine_mask=OC_MASK[k], remote_sem=T.sem.oc,
-                                     src=T.stage[:, d * B:(d + 1) * B], dst=mine))
-        sent += popc(OC_MASK[k])
-    g.remote_dma_fused(trs, local_sem=T.sem.sent)
 
-    oc_total = sum(popc(m) for m in OC_MASK.values())
-    for n, (a, e) in enumerate(near_ranges):
-        qq = q[("sync", "scalar")[n]]
-        qq.wait_ge(T.sem.oc, oc_total)
-        qq.dma_start(T.y[:, a * B:e * B], T.land[:, a * B:e * B]).then_inc(T.sem.st, 16)
-        nst += 1
     for qn, k, c0, c1, ps in STORES:
-        s = far + (i - k) % 4
+        if k == "far":
+            a, e = far * B, (far + 4) * B
+        else:
+            a, e = (far + (i - k) % 4) * B + c0, (far + (i - k) % 4) * B + c1
         for p in ps:
             q[qn].wait_ge(T.sem["a%d" % p], popc(pm[p]) if PIECES[p][0] == "D" else popc(HELP_MASK))
-        q[qn].dma_start(T.y[:, s * B + c0:s * B + c1], T.land[:, s * B + c0:s * B + c1]).then_inc(T.sem.st, 16)
+        q[qn].dma_start(T.y[:, a:e], T.land[:, a:e]).then_inc(T.sem.st, 16)
         nst += 1
 
+    g.wait_ge(T.sem.oc, oc_total)
+    for a, e in near_ranges:
+        g.dma_start(T.y[:, a * B:e * B], T.land[:, a * B:e * B]).then_inc(T.sem.gst, 16)
+    g.wait_ge(T.sem.gst, 16 * len(near_ranges))
     g.wait_ge(T.sem.sent, sent)
     g.wait_ge(T.sem.st, 16 * nst)

from concourse.bass import DstId, RemoteDMATransfer

B = 256

PIECES = [
    ("R", 0, 0, 128),
    ("R", 0, 128, 256),
    ("R", 1, 0, 128),
    ("D", 1, 128, 256),
    ("D", 2, 0, 128),
    ("D", 2, 128, 256),
    ("D", 3, 0, 128),
    ("D", 3, 128, 256),
]
CALLS = [
    [(0, 0x0F), (3, 0x30), (4, 0xC0)],
    [(1, 0x0F), (5, 0x30), (6, 0xC0)],
    [(2, 0x0F), (7, 0xF0)],
    {1: 0x0F00, 2: 0x3000, 3: 0xC000},
]
HELP_MASK = 0xFF
LOADS = [("sync", "far")]
NEAR_Q = ("scalar", "sync")
STORES = [
    ("sync", 2, 0, 256, [4, 5]),
    ("scalar", 0, 0, 256, [0, 1]),
    ("sync", 3, 0, 256, [6, 7]),
    ("scalar", 1, 0, 256, [3, 2]),
]

SCRATCH = {
    "stage": ("sbuf", [128, 2048], "float32"),
    "land": ("sbuf", [128, 2048], "float32"),
}
SEMAPHORES = (["l%d" % k for k in range(4)] + ["a%d" % p for p in range(len(PIECES))]
              + ["lo", "oc", "sent", "st", "gst"])


def popc(m):
    return bin(m).count("1")


def far_calls():
    return [c for c in CALLS if not isinstance(c, dict)]


def piece_mask():
    d = {}
    for call in far_calls():
        for p, m in call:
            d[p] = m
    return d


def helper_of(core):
    return (1 - core // 128) * 128 + 72 + core % 8


def helper_program(g, core, T, topo, s):
    pm = piece_mask()
    hs, i = s // 4, s % 4
    total = 0
    for call in far_calls():
        for p, m in call:
            way, k, c0, c1 = PIECES[p]
            if way != "R":
                continue
            d = 4 * (1 - hs) + (i + k) % 4
            sem = T.sem["a%d" % p]
            g.wait_ge(sem, popc(pm[p]))
            rid, pnc = topo.addr(T.cores[d], core)
            g.remote_dma(out_ap=T.land[:, s * B + c0:s * B + c1], in_ap=T.land[:, d * B + c0:d * B + c1], remote_sem=sem,
                         local_sem=T.sem.sent, pid=pnc, routing_id=rid, dma_engine_mask=HELP_MASK)
            total += popc(HELP_MASK)
    if total:
        g.wait_ge(T.sem.sent, total)


def rank_program(g, core, T, topo):
    rank = T.rank_of(core)
    if rank is None:
        if topo.chip(core) == 9 and core % 8 in (2, 3, 6, 7):
            helper_program(g, core, T, topo, T.rank_of((1 - core // 128) * 128 + 64 + core % 8))
        return
    h, i = rank // 4, rank % 4
    far, near = 4 * (1 - h), 4 * h
    q = {"sync": g.sync, "scalar": g.scalar}
    pm = piece_mask()
    nst = 0

    lsem = {}
    for qn, k in LOADS:
        if k == "far":
            a, e = far * B, (far + 4) * B
            for kk in range(4):
                lsem[kk] = "l0"
        else:
            a = (far + (i + k) % 4) * B
            e = a + B
            lsem[k] = "l%d" % k
        q[qn].dma_start(T.stage[:, a:e], T.x[:, a:e]).then_inc(T.sem[lsem[0 if k == "far" else k]], 16)
    near_ranges = [(a, e) for a, e in ((near, rank), (rank + 1, near + 4)) if e > a]
    for n, (a, e) in enumerate(near_ranges):
        q[NEAR_Q[n]].dma_start(T.stage[:, a * B:e * B], T.x[:, a * B:e * B]).then_inc(T.sem.lo, 16)
    q[NEAR_Q[len(near_ranges) % 2]].dma_start(
        T.y[:, rank * B:(rank + 1) * B], T.x[:, rank * B:(rank + 1) * B]).then_inc(T.sem.st, 16)
    nst += 1

    sent = 0
    oc_total = 0
    have = set()
    mine = T.land[:, rank * B:(rank + 1) * B]
    for call in CALLS:
        trs = []
        if isinstance(call, dict):
            if "lo" not in have:
                g.wait_ge(T.sem.lo, 16 * len(near_ranges))
                have.add("lo")
            for k, m in call.items():
                d = near + (i + k) % 4
                rid, pnc = topo.addr(T.cores[d], core)
                trs.append(RemoteDMATransfer(dst_ids=[DstId(rid=rid, pnc=pnc)], dma_engine_mask=m,
                                             remote_sem=T.sem.oc, src=T.stage[:, d * B:(d + 1) * B], dst=mine))
                sent += popc(m)
                oc_total += popc(m)
            g.remote_dma_fused(trs, local_sem=T.sem.sent)
            continue
        for p, m in call:
            way, k, c0, c1 = PIECES[p]
            if lsem[k] not in have:
                g.wait_ge(T.sem[lsem[k]], 16)
                have.add(lsem[k])
            d = far + (i + k) % 4
            to = T.cores[d] if way == "D" else helper_of(core)
            at = rank if way == "D" else d
            rid, pnc = topo.addr(to, core)
            trs.append(RemoteDMATransfer(dst_ids=[DstId(rid=rid, pnc=pnc)], dma_engine_mask=m,
                                         remote_sem=T.sem["a%d" % p],
                                         src=T.stage[:, d * B + c0:d * B + c1],
                                         dst=T.land[:, at * B + c0:at * B + c1]))
            sent += popc(m)
        g.remote_dma_fused(trs, local_sem=T.sem.sent)

    for qn, k, c0, c1, ps in STORES:
        if k == "far":
            a, e = far * B, (far + 4) * B
        else:
            a, e = (far + (i - k) % 4) * B + c0, (far + (i - k) % 4) * B + c1
        for p in ps:
            q[qn].wait_ge(T.sem["a%d" % p], popc(pm[p]) if PIECES[p][0] == "D" else popc(HELP_MASK))
        q[qn].dma_start(T.y[:, a:e], T.land[:, a:e]).then_inc(T.sem.st, 16)
        nst += 1

    g.wait_ge(T.sem.oc, oc_total)
    for a, e in near_ranges:
        g.dma_start(T.y[:, a * B:e * B], T.land[:, a * B:e * B]).then_inc(T.sem.gst, 16)
    g.wait_ge(T.sem.gst, 16 * len(near_ranges))
    g.wait_ge(T.sem.sent, sent)
    g.wait_ge(T.sem.st, 16 * nst)
